import numpy as np, ml_dtypes
CORES = [35,38,43,46]
N = 4
BF = ml_dtypes.bfloat16
P, V, C, PH, S, Z, CAP, RO = 3072, 1024, 512, 4, 12, 8, 64, 5
I = V // PH
def tail(rng, b, top):
    return np.where(np.arange(16)[:, None] >= rng.integers(0, 17, (N, 8, 1, V)), rng.integers(0, top, b.shape), b)
def parts(rng):
    e = rng.choice(np.array([10.0, 14.0, 18.0, 24.0]), (N, 8, 1, 1))
    x = np.minimum((256 * rng.random((N, 8, 16, P)) ** e).astype(np.int64), 255)
    m = rng.integers(0, 256, (N, 8, 16, V)); b = rng.integers(0, P, (N, 8, 16, V))
    return x, m, b, tail(rng, b, P), rng.integers(0, V, (N, 8, 16, C))
def tops(x, l):
    y = np.take_along_axis(x, l[:, :, 0][:, :, None, :], 3)
    for k in range(1, 16): y = np.maximum(y, np.take_along_axis(x, l[:, :, k][:, :, None, :], 3))
    return y
def late(rng, shape):
    return PH * rng.integers(0, I, shape) + 1 + rng.integers(0, PH - 1, shape)
def pack(x, m, b, d, u):
    r = {"mor": x.reshape(N, 128, P).astype(np.float32).astype(BF), "mea": m.reshape(N, 128, V).astype(np.float32).astype(BF)}
    r["bas"] = b.reshape(N, 128, V).astype(np.int32); r["der"] = d.reshape(N, 128, V).astype(np.int32); r["use"] = u.reshape(N, 128, C).astype(np.int32)
    return r
def setup_inputs(rng):
    x, m, b, d, u = parts(rng); h = rng.integers(0, 8, N)
    for q in range(N):
        g = int(h[q]); x[q, g, :, P - 1] = 255; m[q, g] = rng.integers(0, 151, (16, V)); u[q, g] = late(rng, (16, C))
        d[q, g, rng.integers(0, 16, I), PH * np.arange(I)] = P - 1
    near = rng.random((N, 8, 1, V)) < rng.choice(np.array([0.0, 0.2, 0.5, 0.8]), (N, 8, 1, 1)); near[np.arange(N), h] = False
    m = np.where(near, np.clip(tops(x, d) + rng.integers(-24, 25, m.shape), 0, 255), m)
    for q in range(N):
        for g in range(8):
            v = PH * rng.permutation(I)[:3]; u[q, g][:, b[q, g, 15, v] & (C - 1)] = v
    return pack(x, m, b, d, u)
def setup_inputs_corners(rng):
    x, m, b, d, u = parts(rng); x = np.minimum(x, 100); x[..., P - 1] = 255; m = rng.integers(0, 101, m.shape)
    b = rng.integers(0, P - 1, b.shape); d = tail(rng, b, P - 1); u = late(rng, u.shape)
    u = np.where(rng.random((N, 8, 1, C)) < 0.1, np.where(rng.random((N, 8, 1, C)) < 0.5, V - 1, 1), u); top = tops(x, d)
    for q in range(N):
        for g in range(8):
            if q == 3 and g % 2 == 1:
                n = (0, 1, CAP // 2, CAP - 1)[g // 2]; o = PH * np.arange(I); w = PH * rng.permutation(I) + 1
                m[q, g][:, o] = top[q, g][:, o]; m[q, g][:, w[:n]] = top[q, g][:, w[:n]]
                d[q, g, rng.integers(0, 16, I - n), w[n:]] = P - 1; u[q, g] = PH * rng.integers(0, I, (16, C))
                continue
            n = int(rng.choice(np.array([0, 1, CAP - 1, CAP, CAP + 1, I])))
            if q == 0: n = (CAP, CAP + 1, I, CAP - 1, 1, 0, CAP, CAP + 1)[g]
            if q == 1 or q == 2: n = (CAP, 1, CAP - 1, 0)[g % 4]
            if q == 2 and g == 7: n = CAP + 1
            o = PH * rng.permutation(I); nl = min(n, C // 2); lone, fit, ad = o[:nl], o[nl:n], o[n:]
            cols = 2 * rng.permutation(C // 2)[:nl] + q % 2
            b[q, g, 15, lone] = cols + C * rng.integers(0, P // C - 1, nl); u[q, g][:, cols] = lone
            b[q, g, 15, ad] = 2 * rng.integers(0, C // 2, I - n) + 1 - q % 2 + C * rng.integers(0, P // C - 1, I - n)
            bad = np.concatenate([lone, ad]); d[q, g, rng.integers(0, 16, len(bad)), bad] = P - 1
            m[q, g][:, fit] = top[q, g][:, fit]
            if q == 2:
                o = PH * np.arange(I); z = np.add.reduce(np.arange(1, 17)[:, None] * m[q, g][:, o], axis=0) & (Z - 1)
                left = np.ones(P, dtype=bool); left[P - 1] = False; left[S * np.arange(I) + z] = False
                l = d[q, g][:, o + 1]; l = np.where(left[l], l, rng.choice(np.flatnonzero(left), l.shape))
                d[q, g][:, o + 1] = l; m[q, g][:, o + 1] = np.maximum.reduce(x[q, g][:, l], axis=1)
    return pack(x, m, b, d, u)
def setup_inputs_ties(rng):
    x, m, b, d, u = parts(rng); x[:, 1::2] = x[:, 1::2] >> 6
    k = rng.integers(0, 8, (N, 8, 1, V)); m = np.take_along_axis(m[..., :8], k, 3); m[:, 1::2] = m[:, 1::2] >> 6
    b[:, :2] = np.take_along_axis(b[:, :2, :, :8], k[:, :2], 3); d[:, :2] = np.take_along_axis(d[:, :2, :, :8], k[:, :2], 3)
    lane = np.arange(V); a = rng.integers(40, 81, (N, 16, 1)); high = (np.arange(16)[:, None] == 15) & (lane >= V // 2)
    m[:, 6] = np.where(lane % PH == 0, rng.integers(215, 256, (N, 16, V)), a + high); u[:, 6] = late(rng, (N, 16, C))
    u[..., ::2] = u[:, :, np.arange(16) & 3, ::2]
    return pack(x, m, b, d, u)
def setup_inputs_alike(rng):
    x, m, b, d, u = parts(rng)
    d[:, :3] = b[:, :3]; d[:, 1, 0] = (b[:, 1, 0] + 1) % P; d[:, 2, 15] = (b[:, 2, 15] + 1) % P
    b[:, 3, 15] = rng.integers(0, P, (N, 1)); u[:, 4] = rng.integers(0, V, (N, 1, C))
    for q in range(N):
        v = PH * rng.permutation(I)[:I // 4]; u[q, 4][:, b[q, 4, 15, v] & (C - 1)] = v
    b[:, 5] = rng.integers(0, P, (N, 1, V)); d[:, 5] = rng.integers(0, P, (N, 1, V)); u[:, 6] = (V - 1) * rng.integers(0, 2, (N, 16, C))
    for q in range(N):
        v = PH * rng.permutation(I)[:I // 8]; c = b[q, 7, 15, v] & (C - 1); u[q, 7][:, c] = v; u[(q + 1) % N, 7][:, c] = v
    return pack(x, m, b, d, u)
def setup_inputs_spread(rng):
    x = (np.exp2(8 * rng.random((N, 8, 1, P))) * rng.random((N, 8, 16, P)) ** 3).astype(np.int64)
    m = (np.exp2(8 * rng.random((N, 8, 1, V))) * rng.random((N, 8, 16, V))).astype(np.int64)
    e = rng.choice(np.array([1.0, 2.0, 4.0, 8.0]), (3, N, 8, 1, 1))
    b = (P * rng.random((N, 8, 16, V)) ** e[0]).astype(np.int64); c = (P * rng.random((N, 8, 16, V)) ** e[1]).astype(np.int64)
    d = np.where(np.arange(16)[:, None] >= rng.integers(0, 17, (N, 8, 1, V)), c, b); u = (V * rng.random((N, 8, 16, C)) ** e[2]).astype(np.int64)
    return pack(np.clip(x, 0, 255), np.clip(m, 0, 255), np.clip(b, 0, P - 1), np.clip(d, 0, P - 1), np.clip(u, 0, V - 1))
def setup_inputs_ends(rng):
    def bits(p, n): return 255 * (rng.random((N, 8, 16, n)) < p)
    def lists(n, hi):
        k = rng.random((N, 8, 1, n)); a = hi * rng.integers(0, 2, (N, 8, 16, n))
        return np.where(k < 0.25, 0, np.where(k < 0.5, hi, np.where(k < 0.8, a, rng.integers(0, hi + 1, (N, 8, 16, n)))))
    k = rng.random((N, 8, 1, P)); x = np.where(k < 0.6, 0, np.where(k < 0.63, 255, bits(0.06, P)))
    k = rng.random((N, 8, 1, V)); m = np.where(k < 0.25, 0, np.where(k < 0.5, 255, bits(0.5, V)))
    b = lists(V, P - 1); d = np.where(np.arange(16)[:, None] >= rng.integers(0, 17, (N, 8, 1, V)), lists(V, P - 1), b); u = lists(C, V - 1)
    for t in range(RO):
        for c in (97 * t, 97 * t - 1):
            u[..., c & (C - 1)] = np.where(rng.random((N, 8, 16)) < 0.5, (V - 1) * rng.integers(0, 2, (N, 8, 16)), rng.integers(0, V, (N, 8, 16)))
    x[:, ::2, :, 0] = 255 * rng.integers(0, 2, (N, 4, 16)); x[:, ::2, :, P - 1] = 255 * rng.integers(0, 2, (N, 4, 16)); x[:, 1::2, :, 0] = 0; x[:, 1::2, :, P - 1] = 255
    lo, hi = PH - 1 + PH * (PH % 2), V - 1 - PH
    m[:, 1::2, :, :PH - 1] = 0; m[:, 1::2, :, V - PH:V - 1] = 255; m[..., V - 1] = 255
    m[:, 1::2, :, lo] = 0; m[:, 1::2, :, hi] = 0; m[:, ::2, :, lo] = 255; m[:, ::2, :, hi] = 255
    u[:, 1::2, :, 0] = np.where(np.arange(16) % 2 == 0, 0, V - 1); b[:, 1::2, :, 0] = 0; d[:, 1::2, :, 0] = P - 1
    u[..., C - 1] = np.where(np.arange(16) % 2 == 0, hi, lo)
    b[..., lo] = 0; d[..., lo] = P - 1; b[..., hi] = P - 1; d[..., hi] = 0; d[..., V - 1] = 0
    b[:, :, 15, V - 1] = ((C - 1 - 97 * (PH - 1)) & (C - 1)) + P - C
    return pack(x, m, b, d, u)
def check_inputs(d):
    bad = []
    for k, hi in (("mor", 255), ("mea", 255), ("bas", P - 1), ("der", P - 1), ("use", V - 1)):
        a = np.asarray(d[k]).astype(np.float64)
        if not np.all((a >= 0) & (a <= hi) & (a == np.floor(a))): bad.append("range of " + k)
    return bad
def pick(a, ix):
    return np.stack([np.take(a[g], ix[g], axis=1) for g in range(8)])
def model(kap, mv, own, m, b, d, u):
    c = pick(u, kap)
    s = np.add.reduce(np.abs(pick(m, c) - mv[:, :, None, :]), axis=1)
    k = np.minimum.reduce(np.where(c == own, 2 ** 24, s * 2048 + c), axis=1)
    ok = k < 2 ** 24; w = np.where(ok, k & 2047, 0); dm = pick(d, w)
    diff = pick(b, w) != dm; diff[:, 15] = True
    return ok, w, np.argmax(diff, axis=1), dm
def gap(x, l, mv):
    return np.add.reduce(np.abs(np.maximum.reduce(pick(x, l), axis=2) - mv), axis=1)
def reference(mor, mea, bas, der, use):
    x = mor.astype(np.float32).astype(np.int32).reshape(N, 8, 16, P); m = mea.astype(np.float32).astype(np.int32).reshape(N, 8, 16, V)
    b = bas.astype(np.int32).reshape(N, 8, 16, V); d = der.astype(np.int32).reshape(N, 8, 16, V); u = use.astype(np.int32).reshape(N, 8, 16, C)
    row = np.arange(16)[None, :, None]; i = np.arange(I); count = [0] * N
    for t in range(RO):
        v = PH * i + t % PH; todo = []
        for r in range(N):
            mv = m[r][:, :, v]; bv = b[r][:, :, v]; dv = d[r][:, :, v]; kap = (bv[:, 15] + 97 * t) & (C - 1); mar = count[r] & 127
            ok, w, f, dm = model(kap, mv, v, m[r], b[r], d[r], u[r])
            e = np.where(row < f[:, None, :], bv, dm); old = gap(x[r], dv, mv)
            ad = ok & (gap(x[r], e, mv) + mar < old)
            q = (r + 1 + t % (N - 1)) % N
            sel = np.argsort(ad, axis=1, kind="stable")[:, :CAP]
            asks = ~np.take_along_axis(ad, sel, 1); mv2 = pick(mv, sel)
            ok2, w2, f2, dm2 = model(np.take_along_axis(kap, sel, 1), mv2, -1, m[q], b[q], d[q], u[q])
            e2 = np.where(row < f2[:, None, :], pick(bv, sel), dm2)
            ad2 = asks & (gap(x[r], e2, mv2) + mar < np.take_along_axis(old, sel, 1))
            new = np.where(ad[:, None, :], e, dv); got = ad.copy()
            for g in range(8):
                new[g][:, sel[g][ad2[g]]] = e2[g][:, ad2[g]]; got[g, sel[g][ad2[g]]] = True
            todo.append((ad, w, new, got, (np.add.reduce((row + 1) * mv, axis=1) + t) & (Z - 1)))
        for r in range(N):
            ad, w, new, got, z = todo[r]; d[r][:, :, v] = new; count[r] = int(np.count_nonzero(got))
            for g in range(8):
                j = i[ad[g]]; u[r, g, (j + t) & 15, (j + 37 * t) & (C - 1)] = w[g][j] ^ 1
                j = i[got[g]]; x[r, g][:, S * j + z[g][j]] = m[r, g][:, v[j]]
    return {"yd": d.reshape(N, 128, V).astype(np.float32), "yu": u.reshape(N, 128, C).astype(np.float32), "ym": x.reshape(N, 128, P).astype(np.float32).astype(BF)}

import numpy as np
from concourse.mybir import AluOpType as A, ActivationFunctionType as F

RO, CAP = 5, 64
BIG = float(2 ** 23)
CH = 4
CL = 256 // CH
SPATH = {"1": (3,), "2": (3,)}
UPD = {1: (0, 1, 2), 2: (0, 1, 2, 3), 3: (0, 1)}
SLOT = {}
for _d in UPD:
    for _t in UPD[_d]:
        SLOT[(_d, _t)] = len(SLOT)

SCRATCH = {}


def _b(names, cols, dtype="float32", where="sbuf"):
    for nm in names.split():
        SCRATCH[nm] = (where, [128, cols], dtype)


_b("K1 K2 DD CC WW NN UU DF", 512, "float32", "psum")
_b("morS", 7168, "bfloat16")
_b("meaS neq oneb m16", 1024, "bfloat16")
_b("basI derI", 1024, "int32")
_b("useI", 512, "int32")
_b("basF derF Tt lane nbr", 1024)
_b("useF", 512)
_b("meaQ", 3072, "bfloat16")
_b("useQ", 1536)
_b("TQ", 3072)
_b("lu lt", 256 * len(SLOT))
_b("UN TN", 1024)
_b("mvr", 16384, "bfloat16")
_b("D16", 1024, "uint16")
_b("cl of", 80, "uint16")
_b("XX Y0 Y1 dd1 dd2 aa1 aa2", 4096, "bfloat16")
_b("cU1 cU2 EU1 EU2", 256, "uint16")
_b("cF1 cF2 SS1 SS2 EP1 EP2 val up p1 p2 p3 n4 mbig bigs", 256)
_b("ZB1 ZB2 HH1 HH2 LT1 LT2 LZ LB one If nIf o16 hold", 128)
_b("mu", 64, "uint16")
_b("qi", 256, "int32")
_b("eq ad aE1 aE2 cum zz ad1 got d1 old ge ab junk", 256, "bfloat16")
_b("Ib nIb IB I14 nI14 tmb bo nbo tri k15", 128, "bfloat16")
_b("W8 w8t tm8", 8, "bfloat16")
_b("w64 t64 t65", 64, "bfloat16")
_b("e15 mk8", 64)
_b("RR rr0", 16)
_b("ik8 il8", 64, "int32")
_b("km", 260)
_b("ikm ilm", 260, "int32")
_b("nm bia", 8)
_b("cnt", 1)
_b("pw", 1)

QS = ("V", "S", "P", "G")
SEMAPHORES = list(QS) + ["ld%d" % i for i in range(6)] + ["mc%d" % t for t in range(RO)] + ["st", "sM", "sU", "sT", "sR"]
for _d in UPD:
    SEMAPHORES += ["aM%d" % _d, "aU%d" % _d, "aT%d" % _d]
    for _t in UPD[_d]:
        SEMAPHORES += ["au%d%d" % (_d, _t), "at%d%d" % (_d, _t)]

CY = 1.04e-3
GA = 1.56
START = {"keys2": -21, "scanL1": -50, "D16": -33, "gsel": 62, "act": 28, "cF1": 3, "p1": -14, "gapL2": 13, "delta": 23, "min2": 34, "abs1": 22, "ad1": 34,
         "useQ": 9, "old": 22, "out": -16, "diff": -36, "arrive": -18, "D16n": 33, "cF2": -8, "L1": 28, "E1": -8, "places": 13, "pe": 35, "cU1": 12, "TQ": 26,
         "count": 35, "dmo": 28, "scand2": -22, "D": -26, "load": -10, "scanL2": 9, "tt": 4, "copy": 15, "T": -21, "E2": -39, "gapL1": 34, "keys1": 14, "": 32,
         "send": 31, "mvr": -16, "up": 18, "cum": 26, "basF": -14, "scand1": 29, "L2": 1, "UN": -2, "g": -18, "T0": -22, "gapD": 6, "derF0": -55, "TN": 48,
         "lists": -20, "eq": -2, "useF": 26, "kd": -16, "p2": 27, "cU2": -23, "ts": 36, "neq": -62, "cand1": 8, "scanD": -21, "val": 6, "cand2": -7, "min1": -5,
         "abs2": -25, "got": -1}
FOUND = {}


def rank_program(g, core, T, topo):
    rank = T.rank_of(core)
    if rank is None:
        return
    n = len(T.cores)
    sm = T.sem
    ops, lastw, readers = [], {}, {}

    def op(q, cost, calls, R=(), W=(), sem=None, inc=1, wake=0.0, label="", gat=0.0):
        k = len(ops)
        deps = {}

        def dep(a, kind):
            deps[a] = max(deps.get(a, 0), kind)
        for r in R:
            if r in lastw:
                a = lastw[r]
                dep(a, 1 if r[0] == "!" and q == "P" and ops[a]["q"] == "P" else 2)
            if r[0] == "!":
                for a in readers.get(r, ()):
                    if ops[a]["q"] != q:
                        dep(a, 1)
        for w in W:
            for a in ([lastw[w]] if w in lastw else []) + readers.get(w, []):
                dep(a, 1)
        for r in R:
            readers.setdefault(r, []).append(k)
        for w in W:
            lastw[w] = k
            readers[w] = []
        ops.append({"q": q, "cost": cost, "gat": gat, "calls": calls, "deps": deps, "sem": sem, "inc": inc, "wake": wake, "label": label})
        return k

    def V(c, call, R, W, f=1.0, label=""):
        op("V", 0.06 + max(64.0, c * f) * CY, [call], R, W, label=label, gat=c * CY if f == GA else 0.0)

    def S(c, call, R, W, f=1.0, label=""):
        op("S", 0.09 + c * f * CY, [call], R, W, label=label, gat=c * CY if f == GA else 0.0)

    def P(c, mms, R, W, label="pe"):
        def call(m):
            return lambda e: e.matmul(m[0], m[1], m[2], m[3], m[4])
        op("P", 0.02 + c * 0.85e-3, [call(m) for m in mms], R, W, label=label)

    def G(c, call, R, W, label="g"):
        op("G", 0.2 + 2 * c * CY, [call], R, W, label=label)

    def sel(out, in_, pattern, opc, base, cm, R, W, c, label="gsel"):
        G(c, lambda e: e.affine_select(out, in_, pattern, opc, 0.0, base, cm), R, W, label)

    def gcopy(out, in_, R, W, c, label):
        sel(out, in_, [[0, c]], A.is_ge, 0, 0, R, W, c, label)

    def ts(out, in0, s1, op0, R, W, c, f=1.0, label="ts"):
        V(c, lambda e: e.tensor_scalar(out, in0, s1, None, op0), R, W, f, label)

    def tt(out, a, b, o, R, W, c, f=2.0, label="tt"):
        V(c, lambda e: e.tensor_tensor(out, a, b, o), R, W, f, label)

    def tc(out, a, R, W, c, f=1.0, label="tc"):
        V(c, lambda e: e.tensor_copy(out, a), R, W, f, label)

    def scan(out, d0, d1, o0, o1, R, W, c, f, label):
        V(c, lambda e: e.tensor_tensor_scan(out, d0, d1, 0.0, o0, o1), R, W, f, label)

    def act(out, in_, R, W, c, func=F.Copy, scale=1.0, f=1.0, label="act"):
        S(c, lambda e: e.activation(out, in_, func, scale=scale), R, W, f, label)

    def both(out, in_, R, W, c, label):
        op("VS", 0.08 + c * GA * CY, [(lambda e: e.tensor_copy(out, in_), lambda e: e.activation(out, in_, F.Copy))], R, W, label=label, gat=c * CY)

    def load(qn, i, out, in_, W, us):
        op(qn, 0.1, [lambda e: e.dma_start(out, in_)], (), W, sem="ld%d" % i, inc=16, wake=us, label="load")
    load("Y", 0, T.basI[:], T.bas[:], ["basI"], 3.5)
    load("S", 1, T.meaS[:], T.mea[:], ["meaS"], 3.5)
    load("Y", 2, T.useI[:], T.use[:], ["useI"], 4.0)
    load("Y", 3, T.derI[:], T.der[:], ["derI"], 5.5)
    load("S", 4, T.morS[:, 0:3072], T.mor[:], ["mor"], 8.0)
    load("Y", 5, T.morS[:, 4096:7168], T.mor[:], ["morc"], 10.0)

    V(128, lambda e: e.memset(T.one[:], 1.0), [], ["one"])
    V(512, lambda e: e.memset(T.oneb[:], 1.0), [], ["oneb"])
    V(256, lambda e: e.memset(T.bigs[:], 2.0 * BIG), [], ["bigs"])
    sel(T.e15[:], T.one[:, 0:64], [[-16, 8], [0, 8]], A.is_equal, -15, 1, ["one"], ["e15"], 64)
    G(64, lambda e: e.iota(T.ik8[:], [[0, 8], [-1, 8]], 128, 1), [], ["ik8"])
    sel(T.rr0[:], T.one[:, 0:16], [[-8, 16]], A.is_ge, 0, 1, ["one"], ["rr0"], 16)
    sel(T.RR[:], T.rr0[:], [[8, 16]], A.is_ge, 7, -1, ["rr0"], ["RR"], 16)
    ts(T.il8[:], T.ik8[:], 7, A.bitwise_and, ["ik8"], ["il8"], 64)
    ts(T.mk8[:], T.il8[:], 0.0, A.is_equal, ["il8"], ["mk8"], 64)
    sel(T.If[:], T.one[:], [[-1, 128]], A.is_equal, 0, 1, ["one"], ["If"], 128)
    sel(T.tm8[:], T.oneb[:, 0:8], [[-16, 8]], A.is_ge, 0, 1, ["oneb"], ["tm8"], 8)
    sel(T.w8t[:], T.tm8[:], [[16, 8]], A.is_ge, 15, -1, ["tm8"], ["w8t"], 8)
    act(T.W8[:], T.w8t[:], ["w8t"], ["W8"], 8, scale=2048.0)
    for nm_, sc in (("Ib", 1.0), ("IB", BIG), ("nIb", -1.0), ("nIf", -1.0), ("I14", 16384.0), ("nI14", -32768.0)):
        act(T[nm_][:], T.If[:], ["If"], [nm_], 128, scale=sc)
    act(T.o16[:], T.one[:], ["one"], ["o16"], 128, scale=1.0 / 16)
    sel(T.mbig[:], T.bigs[:], [[0, 16], [1, 16]], A.is_equal, 0, 0, ["bigs"], ["mbig"], 256)
    sel(T.hold[:], T.one[:], [[0, 16], [1, 8]], A.not_equal, 0, 0, ["one"], ["hold"], 128)
    sel(T.m16[:], T.oneb[:], [[0, 64], [1, 16]], A.not_equal, 0, 0, ["oneb"], ["m16"], 1024)
    V(128, lambda e: e.memset(T.ZB1[:], 0.0), [], ["ZB1"])
    V(128, lambda e: e.memset(T.ZB2[:], 0.0), [], ["ZB2"])
    qi = [T.qi[:, 16 * i:16 * i + 16] for i in range(16)]
    G(16, lambda e: e.iota(qi[0], [[0, 16]], 0, 1), [], ["pi"])
    ts(qi[1], qi[0], 15, A.bitwise_and, ["pi"], ["pj"], 16)
    ts(qi[2], qi[1], 12.0, A.mult, ["pj"], ["pk"], 16)
    G(16, lambda e: e.iota(qi[3], [[192, 16]], 0, 0), [], ["s12"])
    tt(qi[4], qi[2], qi[3], A.add, ["pk", "s12"], ["t12"], 16)
    ts(T.pw[:], T.qi[:, 16:17], 1.0, A.add, ["pj"], ["pw"], 1)
    sel(T.t64[:], T.oneb[:, 0:64], [[-16, 8], [0, 8]], A.is_ge, 0, 1, ["oneb"], ["t64"], 64)
    sel(T.t65[:], T.t64[:], [[16, 8], [0, 8]], A.is_ge, 15, -1, ["t64"], ["t65"], 64)
    ts(T.w64[:], T.t65[:], T.pw[:, 0:1], A.mult, ["t65", "pw"], ["w64"], 64)
    sel(T.tmb[:], T.oneb[:, 0:128], [[-16, 8], [0, 16]], A.is_ge, 0, 1, ["oneb"], ["tmb"], 128)
    sel(T.bo[:], T.tmb[:], [[16, 8], [0, 16]], A.is_ge, 15, -1, ["tmb"], ["bo"], 128)
    act(T.nbo[:], T.bo[:], ["bo"], ["nbo"], 128, scale=-1.0)
    sel(T.tmb[:], T.bo[:], [[1, 128]], A.is_ge, 0, -1, ["bo"], ["tmb"], 128)
    act(T.tri[:], T.tmb[:], ["tmb"], ["tri"], 128, scale=8192.0)
    sel(T.tmb[:], T.oneb[:, 0:128], [[0, 8], [1, 16]], A.is_equal, -15, 0, ["oneb"], ["tmb"], 128)
    act(T.k15[:], T.tmb[:], ["tmb"], ["k15"], 128, scale=8192.0)
    G(1024, lambda e: e.iota(T.lane[:], [[1, 1024]], 0, 0, allow_small_or_imprecise_dtypes=True), [], ["lane"])
    G(1024, lambda e: e.iota(T.nbr[:], [[2, 512], [-1, 2]], 1, 0, allow_small_or_imprecise_dtypes=True), [], ["nbr"])
    G(260, lambda e: e.iota(T.ikm[:], [[1, 260]], 128, -1), [], ["ikm"])
    ts(T.ilm[:], T.ikm[:], 15, A.bitwise_and, ["ikm"], ["ilm"], 260)
    ts(T.km[:], T.ilm[:], 0.0, A.is_equal, ["ilm"], ["km"], 260)
    V(1, lambda e: e.memset(T.nm[:, 0:1], 0.0), [], ["nm0"])
    V(1, lambda e: e.memset(T.bia[:, 0:1], 4096.0), [], ["bia"])

    def plus4096(out, in_, R, W, c, label):
        S(c, lambda e: e.activation(out, in_, F.Identity, bias=T.bia[:, 0:1]), R + ["bia"], W, 1.0, label)

    for tau in range(4):
        tc(T.basF[:, tau::4], T.basI[:, tau::4], ["basI"], ["basF%d" % tau], 256, label="basF")
    tc(T.useF[:], T.useI[:], ["useI"], ["useF"], 512, label="useF")
    derall = ["derF%d" % x for x in range(4)]
    for tau in range(4):
        tc(T.D16[:, 256 * tau:256 * tau + 256], T.derI[:, tau::4], ["derI"], ["D16_%d" % tau], 256, label="D16")

    def mvrep(tau, k, q):
        o, i_ = T.mvr[:, 4096 * tau + k:4096 * tau + 4096:16], T.meaS[:, tau::4]
        w = ["mvr%d.%d" % (tau, k)]
        if q == "V":
            tc(o, i_, ["meaS"], w, 256, 0.5, "mvr")
        elif q == "S":
            act(o, i_, ["meaS"], w, 256, label="mvr")
        else:
            gcopy(o, i_, ["meaS"], w, 256, "mvr")
    for k in range(16):
        mvrep(0, k, "S" if k % 3 else "V")
    tt(T.neq[:], T.basI[:], T.derI[:], A.not_equal, ["basI", "derI"], ["neq"], 1024, label="neq")
    tc(T.derF[:], T.derI[:], ["derI"], derall, 1024, label="derF0")
    Th = ["Th0", "Th1"]
    for hf in range(2):
        c0 = slice(512 * hf, 512 * hf + 512)
        bank = ("NN", "UU")[hf]
        P(1024, [(T[bank][:], T.tri[:], T.neq[:, c0], True, False), (T[bank][:], T.k15[0:1, :], T.oneb[0:1, 0:512], False, True)],
          ["tri", "k15", "neq", "oneb"], ["!" + bank])
        plus4096(T.Tt[:, c0], T.derF[:, c0], derall, ["Th%d" % hf], 512, "")
        tt(T.Tt[:, c0], T.Tt[:, c0], T[bank][:], A.min, ["Th%d" % hf, "!" + bank], ["Th%d" % hf], 512, 1.0, "T0")

    def lists(tau):
        P(512, [(T.WW[:, 64 * h:64 * h + 64], T.basF[:, 4 * h + tau::8], T.e15[:], True, True) for h in range(2)], ["basF%d" % tau, "e15"], ["!WW"], "lists")
        for h in range(2):
            tt(T.LB[:, h::2], T.WW[:, 64 * h:64 * h + 64], T.mk8[:], A.mult, ["!WW", "mk8"], ["LB%d" % h], 64, 1.0, "lists")
        P(256, [(T.WW[:, 128:144], T.LB[:], T.RR[:], True, True)], ["LB0", "LB1", "RR"], ["!WW"], "lists")
        for t in [x for x in range(RO) if x % 4 == tau]:
            ts(qi[5], T.WW[:, 128:144], float(97 * t), A.add, ["!WW"], ["q5"], 16, label="lists")
            ts(qi[6], qi[5], 511, A.bitwise_and, ["q5"], ["q6"], 16, label="lists")
            tc(T.cl[:, 16 * t:16 * t + 16], qi[6], ["q6"], ["cl%d" % t], 16, label="lists")

    def places(tau):
        P(128, [(T.WW[:, 64 * h:64 * h + 64], T.meaS[:, 4 * h + tau::8], T.w64[:], True, True) for h in range(2)], ["meaS", "w64"], ["!WW"], "places")
        for h in range(2):
            tt(T.LZ[:, h::2], T.WW[:, 64 * h:64 * h + 64], T.mk8[:], A.mult, ["!WW", "mk8"], ["LZ%d" % h], 64, 1.0, "places")
        P(256, [(T.WW[:, 128:144], T.LZ[:], T.RR[:], True, True)], ["LZ0", "LZ1", "RR"], ["!WW"], "places")
        for t in [x for x in range(RO) if x % 4 == tau]:
            ts(qi[7], T.WW[:, 128:144], float(t), A.add, ["!WW"], ["q7"], 16, label="places")
            ts(qi[8], qi[7], 7, A.bitwise_and, ["q7"], ["q8"], 16, label="places")
            tt(qi[9], qi[8], qi[4], A.add, ["q8", "t12"], ["q9"], 16, label="places")
            tc(T.of[:, 16 * t:16 * t + 16], qi[9], ["q9"], ["of%d" % t], 16, label="places")

    peers = {d: T.cores[(rank - d) % n] for d in UPD}
    common = [e for e in topo.engines(core, peers[1]) if all(e in topo.engines(core, p) for p in peers.values())]
    mask = sum(1 << e for e in common)
    ne = len(common)
    sent, sends = {}, {}

    def send(d, out, in_, asem, lsem, R):
        rid, pid = topo.addr(peers[d])[:2]
        sent[lsem] = sent.get(lsem, 0) + ne
        sends[asem] = len(ops)
        op("G", 0.4, [lambda e: e.remote_dma(out, in_, sm[asem], sm[lsem], pid, rid, mask)], R, (), sem=lsem, inc=0, wake=4.0, label="send")

    def arrive(asem, W, us):
        k = op("R", us, [], (), W, sem=asem, inc=ne, label="arrive")
        ops[k]["deps"][sends[asem]] = 0

    lists(0)
    for d in (1, 2, 3):
        uq, mq, tq = T.useQ[:, 512 * d - 512:512 * d], T.meaQ[:, 1024 * d - 1024:1024 * d], T.TQ[:, 1024 * d - 1024:1024 * d]
        send(d, uq, T.useF[:], "aU%d" % d, "sU", ["useF"])
        send(d, mq, T.meaS[:], "aM%d" % d, "sM", ["meaS"])
        send(d, tq, T.Tt[:], "aT%d" % d, "sT", Th)
        arrive("aU%d" % d, ["useQ%d" % d], 6.0)
        arrive("aM%d" % d, ["meaQ%d" % d], 6.0)
        arrive("aT%d" % d, ["TQ%d.%d" % (d, x) for x in range(4)], 8.0)

    def find(c, t, use, useR, mea, meaR):
        tau = t % 4
        K, cU, cF, dd, aa = T["K" + c], T["cU" + c], T["cF" + c], T["dd" + c], T["aa" + c]
        cl = T.cl[:, 16 * t:16 * t + 16]
        V(256, lambda e: e.tensor_copy(cU[:], use.indirect(cl)), [useR, "cl%d" % t], ["cU" + c], GA, "cU" + c)
        S(256, lambda e: e.activation(cF[:], use.indirect(cl), F.Copy), [useR, "cl%d" % t], ["cF" + c], GA, "cF" + c)
        reps = ["mvr%d.%d" % (tau, k) for k in range(16)]

        def gat(a, b, j):
            return lambda e: e.tensor_tensor(dd[:, a:b], mea.indirect(cU[:, CL * j:CL * (j + 1)]), T.mvr[:, 4096 * tau + a:4096 * tau + b], A.subtract)
        for j in range(CH):
            a, b = 16 * CL * j, 16 * CL * (j + 1)
            dR = "dd%s.%d" % (c, j)
            if j in SPATH[c]:
                act(dd[:, a:b], mea.indirect(cU[:, CL * j:CL * (j + 1)]), [meaR, "cU" + c], [dR], b - a, f=GA, label="scand" + c)
                for a2 in range(a, b, 512):
                    rep = T.mvr[:, 4096 * tau + a2:4096 * tau + a2 + 512]
                    P(1024, [(T.CC[:], T.nIb[:], rep, True, False), (T.CC[:], T.Ib[:], dd[:, a2:a2 + 512], False, True)], ["Ib", "nIb", dR] + reps, ["!CC"], "scand" + c)
                    act(aa[:, a2:a2 + 512], T.CC[:], ["!CC"], ["aa%s.%d" % (c, a2)], 512, F.Abs, label="scand" + c)
                continue
            V(b - a, gat(a, b, j), [meaR, "cU" + c] + reps, [dR], GA, "cand" + c)
            act(aa[:, a:b], dd[:, a:b], [dR], ["aa%s.%d" % (c, x) for x in range(a, b, 512)], b - a, F.Abs, label="abs" + c)
        if c == "1":
            tt(T.eq[:], cF[:], T.lane[:, tau::4], A.is_equal, ["cF1", "lane"], ["eq"], 256, label="eq")
        mm, R, cy = [], ["cF" + c, "If", "W8"] + ["aa%s.%d" % (c, x) for x in range(0, 4096, 512)], 0
        for h in range(2):
            o = K[:, 128 * h:128 * h + 128]
            mm.append((o, cF[:, h::2], T.If[:], True, False))
            cy += 512
            if c == "1":
                mm.append((o, T.eq[:, h::2], T.IB[:], False, False))
                cy += 128
            for k in range(16):
                mm.append((K[:, 128 * h + k:128 * h + 128:16], aa[:, 16 * h + k::32], T.W8[:], False, k == 15))
                cy += 64
        if c == "1":
            R += ["eq", "IB"]
        P(cy, mm, R, ["!K" + c], "keys" + c)
        SS, ZB, HH, LT = T["SS" + c], T["ZB" + c], T["HH" + c], T["LT" + c]
        scan(SS[:], T.mbig[:], K[:, 0:256], A.max, A.min, ["!K" + c, "mbig"], ["SS" + c], 256, 1.0, "min" + c)
        act(ZB[:, 0::8], SS[:, 15::16], ["SS" + c], ["ZB" + c], 16, label="min" + c)
        scan(HH[:], T.hold[:], ZB[:], A.mult, A.add, ["ZB" + c, "hold"], ["HH" + c], 128, 1.0, "min" + c)
        for h in range(2):
            tt(LT[:, h::2], HH[:, 64 * h:64 * h + 64], T.mk8[:], A.mult, ["HH" + c, "mk8"], ["LT%s.%d" % (c, h)], 64, label="min" + c)
        P(256, [(K[:, 256:272], LT[:], T.RR[:], True, True)], ["LT%s.0" % c, "LT%s.1" % c, "RR"], ["!K" + c], "keys" + c)
        mi, mj, m = qi[8 + 2 * int(c)], qi[9 + 2 * int(c)], mu(c, t)
        tc(mi, K[:, 256:272], ["!K" + c], ["mi" + c], 16, label="min" + c)
        ts(mj, mi, 1023, A.bitwise_and, ["mi" + c], ["mj" + c], 16, label="min" + c)
        tc(m[0], mj, ["mj" + c], [m[1]], 16, label="min" + c)

    def mu(c, t):
        k = 2 * int(c) - 2 + t % 2
        return T.mu[:, 16 * k:16 * k + 16], "mu%d" % k

    flip = [0]

    def far(lst, lstR, window, winR, out, outW, tau, label):
        y = flip[0] % 2
        flip[0] += 1
        X, Y = T.XX, T["Y%d" % y]
        for j in range(CH):
            a, b = 16 * CL * j, 16 * CL * (j + 1)
            both(X[:, a:b], window.indirect(lst[:, CL * j:CL * (j + 1)]), [lstR] + winR, ["X.%d" % j], b - a, label)
            scan(Y[:, a:b], T.m16[:, 0:b - a], X[:, a:b], A.mult, A.max, ["X.%d" % j, "m16"], ["Y%d.%d" % (y, j)], b - a, 0.5, "scan" + label)
        P(512, [(T.DF[:, 0:256], T.nIb[:], T.meaS[:, tau::4], True, False), (T.DF[:, 0:256], T.Ib[:], Y[:, 15::16], False, True)],
          ["nIb", "Ib", "meaS"] + ["Y%d.%d" % (y, j) for j in range(CH)], ["!DF"], "diff")
        act(out[:], T.DF[:, 0:256], ["!DF"], [outW], 256, F.Abs, label="gap" + label)

    def own(t):
        find("1", t, T.useF[:], "useF", T.meaS[:], "meaS")

    def ask(t):
        d = 1 + t % 3
        find("2", t, T.useQ[:, 512 * d - 512:512 * d], "useQ%d" % d, T.meaQ[:, 1024 * d - 1024:1024 * d], "meaQ%d" % d)

    def build(c, t, tab, tabR):
        tau = t % 4
        EP, EU = T["EP" + c], T["EU" + c]
        m = mu(c, t)
        V(256, lambda e: e.tensor_tensor(EP[:], tab.indirect(m[0]), T.basF[:, tau::4], A.max), tabR + [m[1], "basF%d" % tau], ["EP" + c], GA, "E" + c)
        tc(EU[:], EP[:], ["EP" + c], ["EU" + c], 256, label="E" + c)

    own(0)
    lists(1)
    places(0)
    places(1)
    for k in range(16):
        mvrep(1, k, "G")
    ask(0)
    lists(2)
    lists(3)
    places(2)
    places(3)
    for tau in (2, 3):
        for k in range(16):
            mvrep(tau, k, "G")

    If, nIf, Ib, nIb = T.If[:], T.nIf[:], T.Ib[:], T.nIb[:]
    D1, D2, N1 = T.DD[:, 0:256], T.DD[:, 256:512], T.NN[:, 0:256]
    W1, W2, U1, U2 = T.WW[:, 0:256], T.WW[:, 256:512], T.UU[:, 0:256], T.UU[:, 256:512]
    done = {}

    def taken(dn, x):
        if (dn, x) in done:
            return
        done[(dn, x)] = 1
        arrive("au%d%d" % (dn, x), ["lu%d%d" % (dn, x)], 5.0)
        arrive("at%d%d" % (dn, x), ["lt%d%d" % (dn, x)], 5.0)
        s = 256 * SLOT[(dn, x)]
        b = 512 * dn - 512 + 37 * x
        gcopy(T.useQ[:, b:b + 256], T.lu[:, s:s + 256], ["lu%d%d" % (dn, x)], ["useQ%d" % dn], 256, "useQ")
        gcopy(T.TQ[:, 1024 * dn - 1024 + x % 4:1024 * dn:4], T.lt[:, s:s + 256], ["lt%d%d" % (dn, x)], ["TQ%d.%d" % (dn, x % 4)], 256, "TQ")

    def rnd(t):
        tau, d, last = t % 4, 1 + t % 3, t + 1 == RO
        nm, nmR = T.nm[:, t:t + 1], "nm%d" % t
        derT, basT, derR, mv = T.derF[:, tau::4], T.basF[:, tau::4], "derF%d" % tau, T.meaS[:, tau::4]
        off = T.of[:, 16 * t:16 * t + 16]
        if t:
            op("Y", 0.1, [lambda e: e.dma_start(T.morS[:, 4096:7168], T.morS[:, 0:3072])], ["mor"], ["morc"], sem="mc%d" % t, inc=16, wake=4.5, label="copy")
        far(T.D16[:, 256 * tau:256 * tau + 256], "D16_%d" % tau, T.morS[:, 0:3072], ["mor"], T.ad, "ad", tau, "D")
        P(256, [(D1, T.nbo[:], T.ad[:], True, False)], ["nbo", "ad"], ["!DD"], "delta")
        build("1", t, T.Tt[:], Th)
        far(T.EU1, "EU1", T.morS[:], ["mor", "morc"], T.aE1, "aE1", tau, "L1")
        P(256, [(D1, T.bo[:], T.aE1[:], False, True)], ["bo", "aE1"], ["!DD"], "delta")
        m = mu("1", t)
        u0 = 37 * t
        useT = T.useF[:, u0:u0 + 256]
        S(256, lambda e: e.activation(T.val[:], T.nbr[:].indirect(m[0]), F.Copy), ["nbr", m[1]], ["val"], GA, "val")
        P(2048, [(U1, If, T.val[:], True, False), (U1, nIf, useT, False, True)], ["If", "nIf", "val", "useF"], ["!UU"], "kd")
        tt(U1, U1, T.km[:, t:t + 256], A.mult, ["!UU", "km"], ["!UU"], 256, 1.0, "kd")
        ts(T.ad1[:], D1, nm, A.is_lt, ["!DD", nmR], ["ad1"], 256, label="ad1")
        tt(T.up[:], U1, T.ad1[:], A.mult, ["!UU", "ad1"], ["up"], 256, 1.0, "up")
        tt(useT, T.up[:], useT, A.add, ["useF", "up"], ["useF"], 256, label="up")
        if not last:
            UN = T.UN[:, 256 * t:256 * t + 256]
            gcopy(UN, useT, ["useF"], ["UN%d" % t], 256, "UN")
            for dn in UPD:
                if t in UPD[dn]:
                    s = 256 * SLOT[(dn, t)]
                    send(dn, T.lu[:, s:s + 256], UN, "au%d%d" % (dn, t), "sR", ["UN%d" % t])
            own(t + 1)
        else:
            op("Y", 0.1, [lambda e: e.dma_start(T.yu[:], T.useF[:])], ["useF"], ["yu"], sem="st", inc=16, wake=4.0, label="out")
        scan(T.cum[:], T.oneb[:, 0:256], T.ad1[:], A.add, A.subtract, ["oneb", "ad1"], ["cum"], 256, 0.5, "cum")
        ts(T.zz[:], T.cum[:], float(CAP), A.is_gt, ["cum"], ["zz"], 256, f=0.5, label="cum")
        P(1024, [(D2, T.I14[:], T.zz[:], True, False), (D2, T.nI14[:], T.ad1[:], False, False), (D2, T.nbo[:], T.ad[:], False, False)],
          ["I14", "nI14", "nbo", "zz", "ad1", "ad"], ["!DD"], "delta")
        S(256, lambda e: e.activation(T.old[:], T.morS[:, 0:3072].indirect(off), F.Copy), ["mor", "of%d" % t], ["old"], GA, "old")
        P(512, [(U2, Ib, mv, True, False), (U2, nIb, T.old[:], False, True)], ["Ib", "nIb", "meaS", "old"], ["!UU"], "dmo")
        build("2", t, T.TQ[:, 1024 * d - 1024:1024 * d], ["TQ%d.%d" % (d, x) for x in range(4)])
        far(T.EU2, "EU2", T.morS[:], ["mor", "morc"], T.aE2, "aE2", tau, "L2")
        P(256, [(D2, T.bo[:], T.aE2[:], False, True)], ["bo", "aE2"], ["!DD"], "delta")
        ts(T.got[:], D2, nm, A.is_lt, ["!DD", nmR], ["got"], 256, label="got")
        tt(T.d1[:], U2, T.got[:], A.mult, ["!UU", "got"], ["d1"], 256, 1.0, "got")
        V(256, lambda e: e.tensor_tensor(T.morS[:, 0:3072].indirect(off), T.d1[:], T.old[:], A.add), ["d1", "old", "of%d" % t], ["mor"], 3.5, "got")
        if last:
            op("Y", 0.1, [lambda e: e.dma_start(T.ym[:], T.morS[:, 0:3072])], ["mor"], ["ym"], sem="st", inc=16, wake=5.0, label="out")
        tt(T.p1[:], T.EP1[:], T.ad1[:], A.mult, ["EP1", "ad1"], ["p1"], 256, label="p1")
        P(1024, [(W1, Ib, T.got[:], True, False), (W1, nIb, T.ad1[:], False, True), (W2, Ib, T.oneb[:, 0:256], True, False), (W2, nIb, T.got[:], False, True)],
          ["Ib", "nIb", "oneb", "got", "ad1"], ["!WW"], "p2")
        tt(T.p2[:], W1, T.EP2[:], A.mult, ["!WW", "EP2"], ["p2"], 256, 1.0, "p2")
        tt(T.p3[:], W2, derT, A.mult, ["!WW", derR], ["p3"], 256, 1.0, "p2")
        P(3072, [(N1, If, T.p1[:], True, False), (N1, If, T.p2[:], False, False), (N1, If, T.p3[:], False, True)], ["If", "p1", "p2", "p3"], ["!NN"], "p2")
        V(256, lambda e: e.tensor_scalar(T.ge[:], N1, 4096.0, -4096.0, A.is_ge, A.mult), ["!NN"], ["ge"], 1.0, "p2")
        tt(derT, N1, T.ge[:], A.add, ["!NN", "ge"], [derR], 256, 1.0, "p2")
        if t == 0:
            tc(T.D16[:, 0:256], T.derF[:, 0::4], ["derF0"], ["D16_0"], 256, label="D16n")
        if last:
            op("Y", 0.1, [lambda e: e.dma_start(T.yd[:], T.derF[:])], derall, ["yd"], sem="st", inc=16, wake=5.0, label="out")
            return
        tt(T.ab[:], basT, derT, A.not_equal, ["basF%d" % tau, derR], ["ab"], 256, label="T")
        plus4096(T.n4[:], derT, [derR], ["n4"], 256, "T")
        P(512, [(N1, T.tri[:], T.ab[:], True, False), (N1, T.k15[0:1, :], T.oneb[0:1, 0:256], False, True)], ["tri", "k15", "oneb", "ab"], ["!NN"], "T")
        tt(T.Tt[:, tau::4], N1, T.n4[:], A.min, ["!NN", "n4"], Th, 256, 1.0, "T")
        TN = T.TN[:, 256 * t:256 * t + 256]
        gcopy(TN, T.Tt[:, tau::4], Th, ["TN%d" % t], 256, "TN")
        for dn in UPD:
            if t in UPD[dn]:
                s = 256 * SLOT[(dn, t)]
                send(dn, T.lt[:, s:s + 256], TN, "at%d%d" % (dn, t), "sR", ["TN%d" % t])
        S(256, lambda e: e.activation(T.junk[:], T.got[:], F.Copy, accum_out=T.cnt[:]), ["got"], ["cnt", "junk"], 1.0, "count")
        P(64, [(T.DF[:, 256:257], T.o16[:], T.cnt[:], True, True)], ["o16", "cnt"], ["!DF"], "count")
        tc(T.qi[:, 224:225], T.DF[:, 256:257], ["!DF"], ["ai"], 1, label="count")
        ts(T.qi[:, 240:241], T.qi[:, 224:225], 127, A.bitwise_and, ["ai"], ["aj"], 1, label="count")
        ts(T.nm[:, t + 1:t + 2], T.qi[:, 240:241], -1.0, A.mult, ["aj"], ["nm%d" % (t + 1)], 1, label="count")
        dn = 1 + (t + 1) % 3
        for x in UPD[dn]:
            if x <= t:
                taken(dn, x)
        ask(t + 1)

    for t in range(RO):
        rnd(t)
    emit(g, sm, ops, sent)


def schedule(ops, bonus, ga, look, lag):
    m = len(ops)
    cost = [o["cost"] + o["gat"] * (ga - GA) for o in ops]
    succ = [[] for _ in range(m)]
    for k, o in enumerate(ops):
        for a in o["deps"]:
            succ[a].append(k)
    prio = [0.0] * m
    for k in range(m - 1, -1, -1):
        o = ops[k]
        best = 0.0
        for s in succ[k]:
            if prio[s] > best:
                best = prio[s]
        prio[k] = best + cost[k] + (0.0 if o["q"] == "R" else o["wake"] + 0.05)
    eff = [prio[k] + bonus.get(ops[k]["label"], 0.0) for k in range(m)]
    left = [len(o["deps"]) for o in ops]
    ready_at = [0.0] * m
    ready = {"V": [], "S": [], "P": [], "G": [], "Y": [], "R": []}
    qs = [("V", "S") if o["q"] == "VS" else (o["q"],) for o in ops]
    where = [""] * m
    for k in range(m):
        if left[k] == 0:
            for q in qs[k]:
                ready[q].append(k)
    free = {q: 0.0 for q in ready}
    end = [0.0] * m
    order = []
    while len(order) < m:
        best = None
        for q, rs in ready.items():
            if not rs:
                continue
            f = free[q]
            s0 = min([ready_at[k] for k in rs])
            s0 = (f if f > s0 else s0) + look
            k, ek = -1, 0.0
            for j in rs:
                if ready_at[j] <= s0 and (k < 0 or eff[j] > ek):
                    if q == "V" and len(qs[j]) == 2 and free["S"] < max(f, ready_at[j]) + lag:
                        continue
                    k, ek = j, eff[j]
            if k < 0:
                continue
            s = f if f > ready_at[k] else ready_at[k]
            if best is None or s < best[0]:
                best = (s, k, q)
        s, k, q = best
        o = ops[k]
        where[k] = q
        for q2 in qs[k]:
            ready[q2].remove(k)
        free[q] = 0.0 if q == "R" else s + cost[k]
        end[k] = s + cost[k] + o["wake"]
        order.append(k)
        for j in succ[k]:
            w = ops[j]["deps"][k]
            r = end[k] + 0.08 if w == 2 or (w == 1 and (q != "P" or ops[j]["q"] != "P")) else s
            if r > ready_at[j]:
                ready_at[j] = r
            left[j] -= 1
            if left[j] == 0:
                for q2 in qs[j]:
                    ready[q2].append(j)
    return order, max(end), where


def find_order(ops, tries=600):
    labels = sorted(set(o["label"] for o in ops))
    rng = np.random.default_rng(7)

    def total(b, lk, lg):
        return sum(schedule(ops, b, ga, lk, lg)[1] for ga in (1.3, 1.8))
    cur = (dict(START), 0.03, 2.4)
    val = best = total(*cur)
    top = cur
    for i in range(tries):
        b, lk, lg = dict(cur[0]), cur[1], cur[2]
        for _ in range(int(rng.integers(1, 3))):
            lb = labels[int(rng.integers(0, len(labels)))]
            b[lb] = float(rng.uniform(-40.0, 40.0)) if rng.random() < 0.5 else b.get(lb, 0.0) + float(rng.normal(0.0, 6.0))
        if rng.random() < 0.1:
            lk = float(rng.uniform(0.0, 0.8))
        if rng.random() < 0.1:
            lg = float(rng.uniform(-1.0, 4.0))
        v = total(b, lk, lg)
        if v <= val + rng.exponential(0.5) * (1.0 - i / tries):
            val, cur = v, (b, lk, lg)
            if v < best:
                best, top = v, cur
    FOUND["best"], FOUND["top"] = best, top
    return schedule(ops, top[0], GA, top[1], top[2])


def emit(g, sem, ops, sent):
    if "order" not in FOUND:
        FOUND["order"], FOUND["span"], FOUND["where"] = find_order(ops)
    where = FOUND["where"]
    eng = {"V": g.vector, "S": g.scalar, "P": g.tensor, "G": g, "Y": g.sync}
    count = {}
    at = {}
    known = {q: {} for q in eng}
    snap = {}
    for k in FOUND["order"]:
        o = ops[k]
        q = where[k]
        if q == "R":
            at[k] = (o["sem"], o["inc"])
            continue
        need = {}
        for a in o["deps"]:
            w = o["deps"][a]
            if w == 2 or (w == 1 and (q != "P" or where[a] != "P")):
                s, v = at[a]
                need[s] = max(need.get(s, 0), v)
        e, kn = eng[q], known[q]
        for s in need:
            v = need[s]
            if kn.get(s, 0) >= v:
                continue
            if any(s2 != s and kn.get(s2, 0) < need[s2] and snap.get((s2, need[s2]), {}).get(s, 0) >= v for s2 in need):
                continue
            e.wait_ge(sem[s], v)
            kn[s] = v
            for s3, v3 in snap.get((s, v), {}).items():
                if kn.get(s3, 0) < v3:
                    kn[s3] = v3
        for s in need:
            if kn.get(s, 0) < need[s]:
                e.wait_ge(sem[s], need[s])
                kn[s] = need[s]
        for c in o["calls"]:
            ins = (c["VS".index(q)] if o["q"] == "VS" else c)(e)
            s = q if o["sem"] is None else o["sem"]
            if o["inc"]:
                count[s] = count.get(s, 0) + o["inc"]
                ins.then_inc(sem[s], o["inc"])
        if o["inc"]:
            at[k] = (s, count[s])
            snap[at[k]] = dict(kn)
        else:
            at[k] = (o["sem"], sent[o["sem"]])
    for s in list(count) + list(sent):
        v = sent[s] if s in sent else count[s]
        if known["Y"].get(s, 0) < v:
            eng["Y"].wait_ge(sem[s], v)
            known["Y"][s] = v
